import numpy as np, ml_dtypes
CORES = [16,18,20,22]
N = 4
BF = ml_dtypes.bfloat16
C, L, S0, K, T, R, Q = 4096, 256, 256, 16, 4, 11, 9
M, S = C // L, S0 + L * T
def perms(rng):
    return np.ascontiguousarray(np.argsort(rng.random((N, 8, S0)), axis=-1))
def parts(rng):
    x = np.floor(rng.random((N, 8, 16, C)) * rng.integers(160, 257, (N, 8, 1, C))).astype(np.int64)
    v = np.floor(rng.random((N, 8, 16, S0)) * rng.integers(96, 257, (N, 8, 1, S0))).astype(np.int64)
    w = rng.integers(0, S0, (N, 8, C)); few = rng.integers(0, S0, (N, 8, 16))
    w = np.where(rng.random((N, 8, C)) < 0.25, np.take_along_axis(few, rng.integers(0, 16, (N, 8, C)), 2), w)
    th = rng.integers(48, 208, (N, 8, 1, T)) + rng.integers(-16, 17, (N, 8, 16, T))
    return x, v, perms(rng), perms(rng), w, th
def pack(x, v, e, h, w, th):
    big = lambda a: np.ascontiguousarray(a.reshape(N, 128, -1)).astype(np.float32).astype(BF)
    return {"x0": big(x), "v0": big(v), "e0": e.astype(np.int32), "h0": h.astype(np.int32), "w0": w.astype(np.int32), "th": big(th)}
def put(p, s, at):
    j = int(np.argmax(p == at)); p[j] = p[s]; p[s] = at
def setup_inputs(rng):
    return pack(*parts(rng))
def setup_inputs_spread(rng):
    x, v, e, h, w, th = parts(rng)
    x = np.floor(np.exp2(8 * rng.random((N, 8, 1, C))) * rng.random((N, 8, 16, C)) * (rng.random((N, 8, 1, C)) > 0.0625)).astype(np.int64)
    v = np.floor(np.exp2(8 * rng.random((N, 8, 1, S0)) * rng.random((N, 8, 1, S0))) * rng.random((N, 8, 16, S0)) * (rng.random((N, 8, 1, S0)) > 0.0625)).astype(np.int64)
    w = np.minimum(np.floor(S0 * rng.random((N, 8, C)) ** 3).astype(np.int64), S0 - 1)
    th = np.floor(np.exp2(8 * rng.random((N, 8, 1, T))) * rng.random((N, 8, 16, T))).astype(np.int64)
    return pack(x, v, e, h, w, th)
def setup_inputs_ends(rng):
    bx = rng.choice(np.array([0.0, 0.1, 0.5, 0.9, 1.0, 1.0]), (N, 8, 1, C)); bv = rng.choice(np.array([0.0, 0.1, 0.5, 0.9, 1.0]), (N, 8, 1, S0))
    bx[:, 7] = rng.choice(np.array([0.0, 0.0, 0.1, 0.1, 1.0]), (N, 1, C)); bx[:, 7, :, ::64] = 0.0
    x = 255 * (rng.random((N, 8, 16, C)) < bx).astype(np.int64); v = 255 * (rng.random((N, 8, 16, S0)) < bv).astype(np.int64)
    w = np.where(rng.random((N, 8, C)) < 0.75, (S0 - 1) * rng.integers(0, 2, (N, 8, C)), rng.integers(0, S0, (N, 8, C)))
    e, h = perms(rng), perms(rng)
    th = 255 * (rng.random((N, 8, 16, T)) < rng.choice(np.array([0.0, 0.25, 0.5, 0.75, 1.0]), (N, 8, 1, T))).astype(np.int64); th[:, 0, :, 0] = 0; th[:, 5, :, T - 1] = 255
    v[..., 0] = 255 * rng.integers(0, 2, (N, 8, 1)); v[..., S0 - 1] = 255 * rng.integers(0, 2, (N, 8, 1))
    v[:, 7, :, 0] = 255; v[:, 7, :, S0 - 1] = 255; w[:, 7] = np.where(((np.arange(C) >> 9) & 1) == 1, 0, S0 - 1)
    v[:, 0, :, 1] = 0; v[:, 0, 15, 1] = 132; v[:, 0, 1, 1] = 1
    v[:, 7, :, L - 2] = 255; v[:, 7, 15, L - 2] = 132; v[:, 7, 13, L - 2] = 254; v[:, 7, 0, L - 2] = 254
    for r in range(N):
        for g in range(8):
            opp = g == 7 or (g & 1) == 0
            put(e[r, g], 0, 0); put(e[r, g], S0 - 1, S0 - 1)
            put(h[r, g], 0, S0 - 1 if opp else 0); put(h[r, g], S0 - 1, 0 if opp else S0 - 1)
        if r & 1: x[r, 6] = 255; v[r, 6] = 0; th[r, 6] = 0
    return pack(x, v, e, h, w, th)
def setup_inputs_corners(rng):
    x, v, e, h, w, th = parts(rng); shift = int(rng.integers(0, 8))
    for r in range(N):
        for g in range(8):
            m = (r + g + shift) & 7; two = rng.permutation(L)[:2]; s1, s2 = int(two[0]), int(two[1])
            if m == 0:
                x[r, g] = 0; v[r, g][:, two] = 255; v[r, g][8, two] = 254; w[r, g] = np.where(((np.arange(C) >> 9) & 1) == 1, s1, s2)
                put(e[r, g], s1, 0); put(e[r, g], s2, 1); put(h[r, g], s1, S0 - 1); put(h[r, g], s2, S0 - 2)
            elif m == 1:
                x[r, g] = rng.integers(0, 100, (16, C)); v[r, g][:, s1] = rng.integers(100, 256, 16); w[r, g] = s1
                put(e[r, g], s1, 0); put(h[r, g], s1, S0 - 1)
            elif m == 2: x[r, g] = 255; v[r, g] = 0; th[r, g] = 0
            elif m == 3: x[r, g] = 255; v[r, g] = 0; v[r, g][:, s1] = 255; th[r, g] = 1
            elif m == 4: w[r, g] = rng.choice(np.array([0, S0 - 1, s1, s2]), C)
            elif m == 5: h[r, g] = e[r, g]
            elif m == 6: h[r, g] = S0 - 1 - e[r, g]
            else: th[r, g] = 255; x[r, g] = np.minimum(x[r, g], 254)
    return pack(x, v, e, h, w, th)
def setup_inputs_crowd(rng):
    x, v, e, h, w, th = parts(rng); o = int(rng.integers(0, N)); other = (o + 1 + int(rng.integers(0, N - 1))) & (N - 1); B = 16 * N
    c = rng.integers(96, 256, (N, 8, 16, 1)); c[:, :, 0] = 255
    d = np.zeros((N, 8, L), np.int64) + ((o - np.arange(N)) & (N - 1))[:, None, None]
    for g, i in ((1, int(rng.integers(0, L))), (5, L - 1)): d[other, g, i] = (d[other, g, i] + 1) & (N - 1)
    z = np.floor(rng.random((N, 8, 16, S0)) * (c + 1)).astype(np.int64)
    z0 = 16 * d + rng.integers(0, 16, (N, 8, L)) - np.sum(z[:, :, 1:, :L] * (2 * np.arange(1, 16) + 1)[:, None], axis=2)
    z[:, :, 0, :L] = (z0 & (B - 1)) + B * rng.integers(0, 256 // B, (N, 8, L))
    return pack(np.zeros_like(x) + c, c - z, e, h, w, th)
def setup_inputs_ties(rng):
    e, h, w = perms(rng), perms(rng), rng.integers(0, S0, (N, 8, C)); one = rng.random((N, 8, 1, 1)) < 0.5; one[:, 0] = True; one[:, 7] = False
    st = np.where(one, 1, 32); v = np.where(one, rng.integers(1, 255, (N, 8, 16, S0)), 32 * rng.integers(1, 7, (N, 8, 16, S0)))
    n = rng.choice(np.array([R - 1] * 12 + [R, 0, 16, R - 1]), (N, 8, 1, C)); less = np.argsort(rng.random((N, 8, 16, C)), axis=2) < n
    x = np.take_along_axis(v, w[:, :, None, :], 3) + st * np.where(less, -1, np.where(rng.random((N, 8, 16, C)) < 0.25, 1, 0))
    th = np.where(one, rng.integers(32, 200, (N, 8, 16, T)), 32 * rng.integers(1, 7, (N, 8, 16, T)))
    return pack(x, v, e, h, w, th)
def check_inputs(d):
    bad = []
    for k, lo, hi in (("x0", 0, 255), ("v0", 0, 255), ("e0", 0, S0 - 1), ("h0", 0, S0 - 1), ("w0", 0, S0 - 1), ("th", 0, 255)):
        a = np.asarray(d[k]).astype(np.float64)
        if not np.all((a >= lo) & (a <= hi) & (a == np.floor(a))): bad.append("range of " + k)
    for k in ("e0", "h0"):
        if not np.all(np.sort(np.asarray(d[k]), axis=-1) == np.arange(S0)): bad.append("permutation " + k)
    return bad
def mark(z):
    return np.sum(z.astype(np.int64) * (2 * np.arange(16) + 1)[:, None], axis=2) & 4095
def reference(x0, v0, e0, h0, w0, th):
    take = np.take_along_axis
    X = x0.astype(np.float32).astype(np.int32).reshape(N, 8, 16, C); W = w0.astype(np.int64)
    V = np.zeros((N, 8, 16, S), np.int32); V[..., :S0] = v0.astype(np.float32).astype(np.int32).reshape(N, 8, 16, S0)
    E = np.full((N, 8, S), -1, np.int64); E[..., :S0] = e0; H = np.full((N, 8, S), -1, np.int64); H[..., :S0] = h0
    thr = th.astype(np.float32).astype(np.int32).reshape(N, 8, 16, T)
    lane = np.arange(L); k = np.arange(K); kap = k * k + k + 1; lower = lane[None, :] < lane[:, None]
    y = V[..., :L] + 0; cur = np.zeros((N, 8, L), np.int64) + lane; A = np.zeros((N, 8), np.int64)
    for t in range(T):
        u = mark(y)
        a = (((u * u) >> 5)[..., None] + kap * u[..., None] + A[:, :, None, None]) & (C - 1)
        a = a.reshape(N, 8, L * K); s = take(W, a, 2)
        xa = take(X, a[:, :, None, :], 3).reshape(N, 8, 16, L, K); vs = take(V, s[:, :, None, :], 3).reshape(N, 8, 16, L, K)
        es = take(E, s, 2).reshape(N, 8, L, K); hs = take(H, s, 2).reshape(N, 8, L, K)
        par = (es < take(E, cur, 2)[..., None]) != (hs < take(H, cur, 2)[..., None])
        hit = par & (np.sum(vs > xa, axis=2) >= R)
        race = np.any(hit, axis=3); f = np.argmax(hit, axis=3)
        ff = f[:, :, None, :, None]; vf = take(vs, ff, 4)[..., 0]; xf = take(xa, ff, 4)[..., 0]
        yn = np.where(race[:, :, None, :], np.abs(vf - xf), np.abs(np.max(xa, axis=4) - y))
        new = np.where(race, take(s.reshape(N, 8, L, K), f[..., None], 3)[..., 0], cur)
        lead = ~race & ~np.any((cur[..., :, None] == cur[..., None, :]) & ~race[..., None, :] & lower, axis=3)
        will = np.sum(yn >= thr[..., t:t + 1], axis=2) >= Q
        for r in range(N):
            for g in range(8):
                i = np.flatnonzero(lead[r, g] & ~will[r, g]); V[r, g][:, cur[r, g, i]] = yn[r, g][:, i]
                i = np.flatnonzero(lead[r, g] & will[r, g]); c = cur[r, g, i]; n = S0 + L * t + i
                V[r, g][:, n] = yn[r, g][:, i]; new[r, g, i] = n
                fe = np.zeros(S, np.int64); fe[E[r, g, c]] = 1; fh = np.zeros(S, np.int64); fh[H[r, g, c]] = 1
                old = np.flatnonzero(E[r, g] >= 0); pe = E[r, g, old]; ph = H[r, g, old]
                E[r, g, old] = pe + (np.add.accumulate(fe) - fe)[pe]; H[r, g, old] = ph + np.add.accumulate(fh)[ph]
                E[r, g, n] = E[r, g, c] + 1; H[r, g, n] = H[r, g, c] - 1
        q = (np.arange(N)[:, None, None] + ((mark(yn) >> 4) & (N - 1))) & (N - 1)
        ya = np.ascontiguousarray(yn[q, np.arange(8)[None, :, None], :, lane[None, None, :]].transpose(0, 1, 3, 2))
        b = M * lane + (mark(ya) & (M - 1))
        np.put_along_axis(X, b[:, :, None, :], ya, 3); np.put_along_axis(W, b, new, 2)
        A = np.sum(race, axis=2); y, cur = yn, new
    return {"yx": X.reshape(N, 128, C).astype(np.float32).astype(BF), "yv": V.reshape(N, 128, S).astype(np.float32).astype(BF), "yw": W.astype(np.float32), "ye": E.astype(np.float32), "yh": H.astype(np.float32)}

import numpy as np
from concourse.bass import DstId, RemoteDMATransfer
from concourse.mybir import dt, AluOpType, AxisListType, ActivationFunctionType
import comms_topo

NL, NK, NCELL, NR, NS = 256, 16, 4096, 4, 1280
NCH = 4
CL = NL // NCH
CJ = CL * NK
DEAD = 4112
TRASH = 4113
VW = 4384
MAGIC = 12582912.0
CYC, PEC, GAT, SCA, WAKE, LAT = 0.001, 0.00085, 1.4, 3.0, 0.12, 2.8
SHORT = 3.0
VR = (0,)

BFT, F32, I32, U16 = "bfloat16", "float32", "int32", "uint16"
SCRATCH, PLACE, SEMAPHORES = {}, {}, ["qv", "qs", "qt", "qg"]
for _n, _w, _d in (
        ("X", NCELL, BFT), ("RT", NCELL, BFT), ("V", VW, BFT), ("RS", 2 * NCELL, BFT), ("XG", NCELL, BFT),
        ("DS", 2 * NCELL, BFT), ("CM", NCELL, BFT), ("DM", NCELL, BFT), ("LOC", 4128, BFT),
        ("Y0", NL, BFT), ("TH", 4, BFT), ("EHI", NL, I32), ("U", NL, I32), ("UT", NL, I32), ("WL", NL, U16),
        ("SR", NL, BFT), ("KB", 2048, BFT), ("KX", 2048, BFT), ("KW", 2048, BFT),
        ("LG", NS, F32), ("GE", NS, F32), ("GH", NS, F32), ("GV", NS, BFT), ("GW", NL, F32)):
    SCRATCH[_n] = ("sbuf", [128, _w], _d)
    PLACE[_n] = (_n, 0, _w, _d)
_at = {BFT: 0, F32: 0, I32: 0, U16: 0}
for _d, _w, _ns in (
        (BFT, NL, "RN0 RN1 ZZ ZF HIT WC LD LDS S1 S2 MM DG DJ NM NMX NMB CKR ZERO LI LI0"),
        (BFT, 128, "DMT BLE BGE B BGQ LTI WMK WM16 WEB WHB WFB WDG WBG ID IDK IDM IDN IDE IDH"),
        (BFT, 128, "M8 M8B N8B CA CB CD2 CE2 WCA WCB ZA ZB YA YB PMA PMB"), (BFT, 32, "ML"),
        (F32, NL, "Y2 SQ X1 X2 JLS MLS MZS WIS CUS HSC COLI RI THL THD T0 T1 PEI SZS SZH PHI PHS NEG LF LM HSQ CRA CRB"),
        (F32, 288, "SZ RE RH"), (F32, 96, "EL"), (F32, 64, "CC CX O2A SPA EA EB"),
        (F32, 32, "BSF ILF TRF JL2 CUM W1 O1 O3 LDL M1 M2 F1 F2 CT CD"),
        (I32, NL, "A1 A2"), (I32, 96, "ELI KI"), (I32, 32, "PI I1 I2 I3 I4"),
        (U16, NL, "LA LB E16"), (U16, 96, "ELU KLU"), (U16, 32, "JLU JL2U VO ZL XL E1L H0L")):
    for _n in _ns.split():
        PLACE[_n] = ("all_" + _d, _at[_d], {32: 16, 96: 80, 288: 264}.get(_w, _w), _d)
        _at[_d] += _w
for _d in _at:
    SCRATCH["all_" + _d] = ("sbuf", [128, _at[_d]], _d)
SCRATCH["EQ"] = ("sbuf", [128, 16, 256], BFT)
PLACE["EQ"] = ("EQ", 0, 4096, BFT)
for _t in range(NR):
    SCRATCH["LAND%d" % _t] = ("sbuf", [128, 4 * NL], BFT)
    PLACE["LAND%d" % _t] = ("LAND%d" % _t, 0, 4 * NL, BFT)
    SEMAPHORES += ["ar%d" % _t, "lo%d" % _t]
for _b in range(8):
    SCRATCH["P%d" % _b] = ("psum", [128, 512], F32)
    PLACE["P%d" % _b] = ("P%d" % _b, 0, 512, F32)
SEMAPHORES += ["dth", "dv", "de", "dwy", "dws", "dx", "oyx", "oyv", "oyw", "oye", "oyh"]

ADD, SUB, MUL, MAX, MIN = AluOpType.add, AluOpType.subtract, AluOpType.mult, AluOpType.max, AluOpType.min
GE, GT, LE, LT, EQL = AluOpType.is_ge, AluOpType.is_gt, AluOpType.is_le, AluOpType.is_lt, AluOpType.is_equal
SHR, AND = AluOpType.logical_shift_right, AluOpType.bitwise_and
COPY, IDENT = ActivationFunctionType.Copy, ActivationFunctionType.Identity
ABS, SQUARE = ActivationFunctionType.Abs, ActivationFunctionType.Square


def rank_program(g, core, T, topo):
    rank = T.rank_of(core)
    if rank is None:
        return
    N = len(T.cores)
    Q = {"v": g.vector, "s": g.scalar, "t": g.tensor, "g": g, "y": g.sync}
    nodes, hist, bank = [], {}, {}

    def view(n, lo=0, hi=None, step=1, ind=None, ap=None):
        phys, off, w, d = PLACE[n]
        if hi is None:
            hi = w
        if ap is None:
            ap = T[phys][:, off + lo:off + hi:step] if step > 1 else T[phys][:, off + lo:off + hi]
            if ind is not None:
                p2, o2 = PLACE[ind[0]][:2]
                ap = ap.indirect(T[p2][:, o2 + ind[1]:o2 + ind[2]])
        n_el = 16 * (ind[2] - ind[1]) if ind is not None else -((lo - hi) // step)
        return {"n": n, "lo": lo, "hi": hi, "ap": ap, "ind": ind, "el": n_el, "b2": d in (BFT, U16), "ps": n[0] == "P" and n[1:].isdigit()}

    def node(q, calls, rd, wr, cost, sem=None, lat=0.0, wait=None):
        i = len(nodes)
        real, order = set(), set()
        for v, w in [(v, False) for v in rd] + [(v, True) for v in wr]:
            spans = [(v["n"], v["lo"], v["hi"], w)]
            if v["ind"] is not None:
                spans.append((v["ind"][0], v["ind"][1], v["ind"][2], False))
            for (n, lo, hi, ww) in spans:
                if n[0] == "P" and n[1:].isdigit():
                    b = bank.setdefault(n, [None, None, None])
                    if b[0] == q:
                        if b[1] != i:
                            order.add(b[1])
                        if b[2] is not None:
                            real.add(b[2])
                        b[1] = i
                    else:
                        if b[1] is not None:
                            real.add(b[1])
                        b[0], b[1], b[2] = q, i, b[1]
                    continue
                h = hist.setdefault(n, [])
                real.update(e[3] for e in h if (ww or e[2]) and e[0] < hi and lo < e[1] and e[3] != i)
                if ww:
                    h = [e for e in h if not (lo <= e[0] and e[1] <= hi)]
                h.append((lo, hi, ww, i))
                hist[n] = h
        nodes.append({"q": q, "calls": calls, "real": real, "order": order - real, "cost": cost, "sem": sem, "lat": lat, "wait": wait})
        return i

    def flush():
        n = len(nodes)
        succ = [[] for _ in range(n)]
        for i, x in enumerate(nodes):
            for p in x["real"] | x["order"]:
                succ[p].append(i)
        prio = [0.0] * n
        for i in range(n - 1, -1, -1):
            prio[i] = nodes[i]["cost"] + nodes[i]["lat"] + max([prio[j] + WAKE for j in succ[i]] + [0.0])
        left = [len(x["real"] | x["order"]) for x in nodes]
        ready = {q: [] for q in Q}
        rt = [0.0] * n
        free = {q: 0.0 for q in Q}
        for i in range(n):
            if left[i] == 0:
                ready[nodes[i]["q"]].append(i)
        seq, end = [], [0.0] * n
        while len(seq) < n:
            best = None
            for q in Q:
                if not ready[q]:
                    continue
                e = min(max(free[q], rt[i]) for i in ready[q])
                i = max((i for i in ready[q] if max(free[q], rt[i]) <= e + 0.02),
                        key=lambda i: (prio[i] + (SHORT if nodes[i]["cost"] < 1 else 0), -i))
                k = (max(free[q], rt[i]), -prio[i])
                if best is None or k < best[0]:
                    best = (k, q, i)
            q, i = best[1], best[2]
            ready[q].remove(i)
            seq.append(i)
            free[q] = best[0][0] + nodes[i]["cost"]
            end[i] = free[q] + nodes[i]["lat"]
            for j in succ[i]:
                w = 0.05 if nodes[j]["q"] == q and not nodes[i]["lat"] else WAKE
                if i in nodes[j]["order"]:
                    w = 0.0
                rt[j] = max(rt[j], end[i] + w)
                left[j] -= 1
                if left[j] == 0:
                    ready[nodes[j]["q"]].append(j)
        total, clocks, known, at = {}, {}, {q: {} for q in Q}, {}

        def learn(q, key, cnt):
            k = known[q]
            if k.get(key, 0) < cnt:
                Q[q].wait_ge(T.sem[key], cnt)
                k[key] = cnt
                for kk, nn in clocks[(key, cnt)].items():
                    if k.get(kk, 0) < nn:
                        k[kk] = nn
        for i in seq:
            x = nodes[i]
            q = x["q"]
            need = {}
            for p in x["real"]:
                if at[p] is not None:
                    need[at[p][0]] = max(need.get(at[p][0], 0), at[p][1])
            for key in sorted(need, key=lambda key: -need[key]):
                learn(q, key, need[key])
            if x["wait"] is not None:
                Q[q].wait_ge(T.sem[x["wait"][0]], x["wait"][1])
            key = x["sem"] or "q" + q
            if key == "none":
                x["calls"][0]()
                at[i] = None
                continue
            for k, call in enumerate(x["calls"]):
                ins = call()
                if key[0] != "q":
                    ins.then_inc(T.sem[key], 16)
                    total[key] = total.get(key, 0) + 16
                elif k == len(x["calls"]) - 1:
                    ins.then_inc(T.sem[key], 1)
                    total[key] = total.get(key, 0) + 1
            at[i] = (key, total[key])
            c = dict(known[q])
            c[key] = total[key]
            clocks[at[i]] = c
        for key in sorted(total):
            learn("g", key, total[key])

    def sc(x):
        return x["ap"] if isinstance(x, dict) else x

    def scr(*xs):
        return [x for x in xs if isinstance(x, dict)]

    def cy(n):
        return 0.02 + CYC * max(64, n)

    def half(*vs):
        return cy(vs[0]["el"] * (0.5 if all(v["b2"] for v in vs) else 1))

    def ts(out, i0, s1, op0, s2=None, op1=None):
        if op1 is None:
            node("v", [lambda: g.vector.tensor_scalar(out["ap"], i0["ap"], sc(s1), None, op0)], [i0] + scr(s1), [out], half(out, i0))
        else:
            node("v", [lambda: g.vector.tensor_scalar(out["ap"], i0["ap"], sc(s1), sc(s2), op0, op1)], [i0] + scr(s1, s2), [out], half(out, i0))

    def tt(out, a, b, op):
        c = 0.06 + CYC * GAT * out["el"] if a["ind"] else cy(out["el"] * (1 if a["ps"] or b["ps"] else 2))
        node("v", [lambda: g.vector.tensor_tensor(out["ap"], a["ap"], b["ap"], op)], [a, b], [out], c)

    def tc(out, a):
        c = 0.06 + CYC * GAT * out["el"] if a["ind"] else 0.06 + CYC * SCA * out["el"] if out["ind"] else half(out, a)
        node("v", [lambda: g.vector.tensor_copy(out["ap"], a["ap"])], [a], [out], c)

    def ms(out, c):
        node("v", [lambda: g.vector.memset(out["ap"], c)], [], [out], half(out))

    def scan(out, a, b, init, op0, op1):
        node("v", [lambda: g.vector.tensor_tensor_scan(out["ap"], a["ap"], b["ap"], init, op0, op1)], [a, b], [out], half(out, a, b))

    def act(out, a, func=COPY, bias=None, scale=None, wait=None):
        kw = {}
        if bias is not None:
            kw["bias"] = sc(bias)
        if scale is not None:
            kw["scale"] = sc(scale)
        c = 0.08 + CYC * GAT * out["el"] if a["ind"] else cy(a["el"])
        node("s", [lambda: g.scalar.activation(out["ap"], a["ap"], func, **kw)], [a] + scr(bias, scale), [out], c, wait=wait)

    def mms(out, pairs, start=True, stop=True):
        n = len(pairs)

        def one(k, l, r):
            return lambda: g.tensor.matmul(out["ap"], l["ap"], r["ap"], start and k == 0, stop and k == n - 1)
        node("t", [one(k, l, r) for k, (l, r) in enumerate(pairs)], [x for p in pairs for x in p], [out], n * (0.01 + PEC * max(64, out["el"])))

    def mm(out, l, r, start=True, stop=True):
        mms(out, [(l, r)], start, stop)

    def gio(out, pat, base, cm=0):
        kw = {} if PLACE[out["n"]][3] == I32 else {"allow_small_or_imprecise_dtypes": True}
        node("g", [lambda: g.iota(out["ap"], pat, base, cm, **kw)], [], [out], 0.15 + 2 * CYC * out["el"])

    def dma(q, pairs, sem, rd, wr, us=2.0):
        node(q, [(lambda o=o, i=i: Q[q].dma_start(o, i)) for o, i in pairs], rd, wr, 0.06 * len(pairs), sem, us)

    def kset(n, k):
        return view(n, 128 * k, 128 * k + 128)

    def every16(n):
        return view(n, 15, NL, 16)

    def lanes(pn, w, src, mask, out):
        mm(view(pn, 0, NL), view("ID"), view(mask), True, False)
        mm(view(pn, 0, NL), view(w), src, False, True)
        scan(view(out), view("DJ"), view(pn, 0, NL), 0.0, MUL, MAX)

    ms(view("EHI"), 0)
    gio(view("PI", 0, 1), [[1, 1]], 0, 1)
    gio(view("COLI"), [[1, NL]], 0)
    gio(view("RI"), [[0, 16], [1, 16]], 0)
    wl = [[(T.U[:, 32 * ip + 16 * ga:32 * ip + 16 * ga + 16], T.w0[ga::2, 512 * ip:512 * ip + 512]) for ip in range(8)] for ga in range(2)]
    dma("s", [(T.Y0[:, :], T.v0[:, :])], "dv", [], [view("Y0")])
    dma("y", wl[0], "dwy", [], [view("U", 0, 8)], 3.0)
    dma("s", wl[1], "dws", [], [view("U", 8, NL)], 3.0)
    dma("y", [(T.EHI[0::16, :], T.e0[:, :]), (T.EHI[1::16, :], T.h0[:, :])], "de", [], [view("EHI")])
    dma("y", [(T.X[:, :], T.x0[:, :])], "dx", [view("U"), view("Y0")], [view("X")], 6.0)
    dma("y", [(T.TH[:, :], T.th[:, :])], "dth", [], [view("TH")], 6.0)
    gio(view("V", 0, DEAD), [[0, DEAD]], -1)
    gio(view("V", DEAD, VW), [[0, VW - DEAD]], 0)
    gio(view("DM"), [[0, 256], [16384, 16]], 0)
    gio(view("RS", NCELL, 2 * NCELL), [[0, NCELL]], 0)
    gio(view("ZERO"), [[0, NL]], 0)
    gio(view("CT", 0, 4), [[1, 4]], 1)
    for t in range(NR):
        gio(view("CD", t, t + 1), [[0, 1]], 2 ** (3 - t))
    gio(view("SZ"), [[0, 264]], 0)
    gio(view("RE"), [[0, 264]], -1)
    gio(view("RH"), [[0, 264]], -1)
    gio(view("NEG"), [[0, NL]], -5)
    gio(view("LOC", 0, 16), [[0, 16]], 0)
    gio(view("LOC", DEAD, DEAD + 16), [[0, 16]], 0)

    def cc(j):
        return view("CC", j, j + 1)

    def cx(j):
        return view("CX", j, j + 1)
    PQ, NP16, PF, WM, WE_, WH_, WF, KAP, KEEP, WWC, Q16, R3, R0, R2, R4, LO, NLO, BLO, QM8, QP8, L32, H32 = range(22)
    A = [view("CC", 40 + t, 41 + t) for t in range(NR)]
    ts(view("PI", 2, 3), view("PI", 0, 1), 15, AND)
    ts(view("PI", 4, 5), view("PI", 0, 1), 4, SHR)
    tc(cc(PQ), view("PI", 2, 3))
    ts(cc(NP16), view("PI", 4, 5), -16.0, MUL)
    tc(cc(PF), view("PI", 0, 1))
    ts(view("DMT"), view("COLI", 0, 128), cc(NP16), ADD)
    ts(view("BLE"), view("DMT"), 15.0, LE)
    ts(view("BGE"), view("DMT"), 0.0, GE)
    ts(cc(WM), cc(PQ), 2.0, MUL, 1.0, ADD)
    tt(view("B"), view("BLE"), view("BGE"), MUL)
    ts(view("WMK"), view("B"), cc(WM), MUL)
    ts(cx(0), cc(PQ), 0.0, EQL, -2048.0, MUL)
    ts(cx(1), cc(PQ), 1.0, EQL, 0.5, MUL)
    tt(cx(2), cx(0), cx(1), ADD)
    ts(view("CKR"), view("RI"), 0.0, MUL, cx(2), ADD)
    ts(view("ID"), view("COLI", 0, 128), cc(PF), EQL)
    ts(view("IDM"), view("ID"), -4096.0, MUL)
    ts(cx(3), cc(PQ), cc(PQ), MUL, 1.0, ADD)
    tt(cc(KAP), cx(3), cc(PQ), ADD)
    ms(A[0], 0.0)
    for k in range(16):
        ts(kset("KB", k), view("DMT"), float(k), EQL)
    for r, j in ((0, R0), (2, R2), (3, R3), (4, R4)):
        ts(cc(j), cc(PQ), float(r), EQL)
    ts(view("LI"), view("COLI"), cc(R3), MUL)
    ts(view("LI0"), view("LI"), cc(R0), ADD)
    ts(cx(4), cc(R0), 16.0, MUL)
    tt(cc(WE_), cx(4), cc(R2), ADD)
    ts(cx(6), cc(PQ), 1.0, EQL, 16.0, MUL)
    tt(cc(WH_), cx(6), cc(R2), SUB)
    ts(view("IDE"), view("ID"), cc(WE_), MUL)
    ts(view("IDH"), view("ID"), cc(WH_), MUL)
    for j in range(4):
        j2 = (j + 2) % 4
        pj = view("P%d" % (2 + j), 0, 512)
        mms(pj, [(view("IDE"), view("KB", 512 * j, 512 * j + 512)), (view("IDH"), view("KB", 512 * j2, 512 * j2 + 512))])
        act(view("KX", 512 * j, 512 * j + 512), pj)
    ts(cc(LO), cc(PQ), 8.0, LT)
    ts(cc(NLO), cc(LO), -8192.0, MUL)
    ts(cc(BLO), cc(LO), 8193.0, MUL, -1.0, ADD)
    ts(view("M8"), view("RI", 0, 128), 8.0, LT)
    tt(view("M8B"), view("B"), view("M8"), MUL)
    tt(view("N8B"), view("B"), view("M8B"), SUB)
    ts(view("CA"), view("M8B"), cc(WE_), MUL)
    ts(view("CB"), view("N8B"), cc(WH_), MUL)
    tt(view("WCA"), view("CA"), view("CB"), ADD)
    ts(view("CD2"), view("M8B"), cc(WH_), MUL)
    ts(view("CE2"), view("N8B"), cc(WE_), MUL)
    tt(view("WCB"), view("CD2"), view("CE2"), ADD)
    ts(cx(10), cc(LO), 999.0, MUL, -8.0, ADD)
    tt(cc(QM8), cc(PQ), cx(10), ADD)
    ts(cx(11), cc(LO), -999.0, MUL, 1007.0, ADD)
    tt(cc(QP8), cc(PQ), cx(11), ADD)
    ts(cc(L32), cc(LO), 32.0, MUL)
    ts(cc(H32), cc(LO), -32.0, MUL, 32.0, ADD)
    ts(view("ZA"), view("DMT"), cc(QM8), EQL, 32.0, MUL)
    ts(view("ZB"), view("DMT"), cc(QP8), EQL, 32.0, MUL)
    ts(view("YA"), view("ID"), cc(L32), MUL)
    ts(view("YB"), view("ID"), cc(H32), MUL)
    tt(view("PMA"), view("YA"), view("ZA"), ADD)
    tt(view("PMB"), view("YB"), view("ZB"), ADD)
    ts(view("WEB"), view("B"), cc(WE_), MUL)
    ts(view("WHB"), view("B"), cc(WH_), MUL)
    ts(view("DG"), view("RI"), cc(PQ), EQL)
    ts(view("T0"), view("DG"), 8192.0, MUL)
    ts(view("NM"), view("T0"), -8192.0, ADD)
    ts(view("NMX"), view("NM"), 256.0, MUL)
    ms(view("DJ"), 1.0)
    ms(view("DJ", 0, NL, 16), 0.0)
    ts(view("IDN"), view("ID"), -1.0, MUL)
    ts(view("BGQ"), view("DMT"), cc(PQ), GE)
    tt(view("LTI"), view("BLE"), view("BGQ"), MUL)
    ts(cx(7), cc(PQ), 15.0, EQL, 4095.0, MUL)
    ts(cc(WF), cx(7), 1.0, ADD)
    ts(view("WFB"), view("B"), cc(WF), MUL)
    ts(view("T1"), view("COLI"), 16.0, MUL, 8192.0, ADD)
    tt(view("HSC"), view("T1"), view("DG"), MUL)
    ts(view("NMB"), view("HSC"), -8192.0, ADD)
    ts(view("WM16"), view("WMK"), 16.0, MUL)
    ts(cc(Q16), cc(PQ), 16.0, MUL)
    ts(view("BSF"), view("COLI", 0, 16), 256.0, MUL, cc(Q16), ADD)
    ts(view("ILF"), view("COLI", 0, 16), 16.0, MUL, cc(PQ), ADD)
    ts(view("TRF"), view("ILF"), float(TRASH), ADD)
    ts(cc(KEEP), cc(PQ), 2.0, LE)
    ts(view("IDK"), view("ID"), cc(KEEP), MUL)
    ts(view("CT", 4, 8), view("CT", 0, 4), cc(R4), MUL)
    ts(view("CD", 4, 8), view("CD", 0, 4), cc(R2), MUL)
    tt(view("CT", 8, 12), view("CT", 4, 8), view("CD", 4, 8), ADD)
    ts(view("CX", 20, 36), view("COLI", 0, 16), cc(PQ), ADD, 15.0, LT)
    ts(view("CX", 36, 52), view("CX", 20, 36), 1.0, ADD)
    scan(view("PEI", 0, 16), view("CX", 36, 52), view("CX", 36, 52), 1.0, MUL, MAX)
    ts(view("WDG"), view("B"), view("PEI", 15, 16), MUL)
    ts(view("WBG"), view("B"), 65536.0, MUL)
    ts(view("SZS"), view("DJ"), 0.5, MUL)
    ts(view("SZH"), view("DJ"), 0.0, EQL, 65536.0, MUL)
    scan(view("THL"), view("SZS"), view("SZH"), 0.0, MUL, MAX)
    tt(view("THD"), view("THL"), view("DG"), MUL)
    ts(cx(9), cc(R4), 256.0, MUL)
    tt(cc(WWC), cx(9), cc(R3), ADD)
    act(view("KW"), view("KB"), COPY, scale=cc(WWC))
    tt(view("SR"), view("EHI"), view("LI0"), ADD)

    def cells(y, more, a):
        mms(view("P0", 0, NL), [(view("B"), view("CKR")), (view("WMK"), y)])
        mm(view("P1", 0, NL), view("WMK"), y, True, False)
        act(view("Y2"), view("P0", 0, NL), IDENT, bias=MAGIC, scale=1.0 / 4096)
        act(view("MM"), view("Y2"), IDENT, bias=-MAGIC)
        mm(view("P1", 0, NL), view("IDM"), view("MM"), False, True)
        act(view("SQ"), view("P1", 0, NL), SQUARE)
        act(view("X1"), view("SQ"), IDENT, bias=-0.4375, scale=1.0 / 32)
        act(view("X2"), view("X1"), IDENT, bias=MAGIC + more)
        act(view("P0", 0, NL), view("P1", 0, NL), IDENT, bias=a, scale=cc(KAP))
        tt(view("A1"), view("X2"), view("P0", 0, NL), ADD)
        ts(view("A2"), view("A1"), 4095, AND)
        tc(view("LA"), view("A2"))

    def current(rec):
        mm(view("P6", 0, NL), view("WEB"), view(rec))
        tc(view("E16"), view("P6", 0, NL))
        lanes("P5", "WEB", view(rec), "NM", "CUS")
        for n, w, o in (("CRA", "WCA", 0), ("CRB", "WCB", NL)):
            mm(view("P7", o, o + NL), view(w), view(rec))
            act(view(n), view("P7", o, o + NL))

    cells(view("Y0"), 0.0, A[0])
    node("v", [lambda: g.vector.transpose(T.UT[:, :], T.U[:, :])], [view("U")], [view("UT")], cy(NL))
    tc(view("WL"), view("UT"))
    for c in range(4):
        (tc if c % 2 else act)(view("RT", 1024 * c, 1024 * c + 1024), view("SR", 0, NL, 1, ("WL", 64 * c, 64 * c + 64)))
    current("SR")
    tc(view("EL", 0, 16), every16("CUS"))
    tc(view("VO"), every16("CUS"))
    tc(view("V", 0, VW, 1, ("VO", 0, 16)), view("Y0"))
    ts(view("E1L"), view("EL", 0, 16), 0.0625, MUL)
    lanes("P7", "WHB", view("SR"), "NM", "PHS")
    ts(view("H0L"), every16("PHS"), 0.0625, MUL)

    rec = "SR"
    y = view("Y0")
    for t in range(NR):
        newrec = "RN%d" % (t % 2)
        land = "LAND%d" % t
        O2 = view("O2A", 16 * t, 16 * t + 16)
        SP = view("SPA", 16 * t, 16 * t + 16)
        more = t + 1 < NR

        def ch(n, c):
            return view(n, CL * c, CL * c + CL)

        def cj(n, c, off=0):
            return view(n, off + CJ * c, off + CJ * c + CJ)

        def cand(n, c, k, off=0):
            return view(n, off + CJ * c + k, off + CJ * c + CJ, 16)

        for c in range(NCH):
            (tc if c in VR else act)(cj("RS", c), view("RT", 0, NCELL, 1, ("LA", CL * c, CL * c + CL)))
            act(cj("XG", c), view("X", 0, NCELL, 1, ("LA", CL * c, CL * c + CL)))
            pa, pb = view("P%d" % (c % 2), 0, CL), view("P%d" % (2 + c % 2), 0, CL)
            pc, pn = view("P%d" % (7 if c % 2 else 4), 0, CL), view("P5", 0, CL)
            mms(pa, [(kset("KX", k), cand("RS", c, k)) for k in range(8)])
            mms(pb, [(kset("KX", k), cand("RS", c, k)) for k in range(8, 16)])
            act(ch("LF", c), pa, IDENT, bias=cc(BLO), scale=cc(LO))
            tt(ch("LM", c), ch("LF", c), pb, MAX)
            ts(ch("LB", c), ch("LM", c), cc(NLO), ADD)
            tt(ch("S1", c), pa, ch("CRA", c), LT)
            tt(ch("S2", c), pb, ch("CRB", c), LT)
            tt(cj("DS", c), view("V", 0, VW, 1, ("LB", CL * c, CL * c + CL)), cj("XG", c), SUB)
            ts(cj("CM", c), cj("DS", c), 0.0, GT)
            scan(cj("DS", c, NCELL), cj("DM", c), cj("XG", c), 0.0, MIN, MAX)
            mms(pc, [(view("PMA"), ch("S1", c)), (view("PMB"), ch("S2", c))] + [(kset("KB", k), cand("CM", c, k)) for k in range(16)])
            act(ch("HSQ", c), pc, SQUARE, bias=-45.5)
            ts(ch("HIT", c), ch("HSQ", c), 9.0, LE)
            mm(pn, view("LTI"), ch("HIT", c))
            ts(ch("ZF", c), pn, 0.0, EQL)
            mms(pn, [(view("ID"), ch("NMB", c)), (view("WFB"), ch("ZF", c))])
            scan(ch("JLS", c), ch("DJ", c), pn, 0.0, MUL, MAX)
            mms(view("P6", 0, CL), [(view("IDN"), view(y["n"], CL * c, CL * c + CL)), (view("ID"), cand("DS", c, 15, NCELL))])
            act(cand("DS", c, 15, NCELL), view("P6", 0, CL))
        act(view("RS", NCELL + 15, 2 * NCELL, 16), view(rec))
        mms(view("P6", 0, NL), [(view("IDK"), view(rec)), (view("ID"), view("LI"))])
        act(view("RS", NCELL + 14, 2 * NCELL, 16), view("P6", 0, NL), IDENT, bias=view("CT", 8 + t, 9 + t))
        tc(view("JLU"), every16("JLS"))
        ynew = view(land, 0, NL)
        act(ynew, view("DS", 0, 2 * NCELL, 1, ("JLU", 0, 16)), ABS)

        dsts, ids = [], []
        for j in range(1, N):
            r = (rank + j) % N
            d = (rank - r) % N
            a = topo.addr(T.cores[r])
            ids.append(DstId(rid=a[0], pnc=a[1]))
            dsts.append(T[land][:, d * NL:(d + 1) * NL])
        msk = topo.mask(core, T.cores[(rank + 1) % N])
        neng = len(topo.engines(core, T.cores[(rank + 1) % N]))

        def send(ids=ids, dsts=dsts, msk=msk, t=t, src=ynew["ap"]):
            return g.remote_dma_fused([RemoteDMATransfer(dst_ids=ids, dma_engine_mask=msk, remote_sem=T.sem["ar%d" % t],
                                                         src=src, dsts=dsts)], local_sem=T.sem["lo%d" % t])
        node("g", [send], [ynew], [view(land, NL, 4 * NL)], 0.1, "none", LAT)

        ts(view("ML"), every16("JLS"), 4096.0, GE)
        tt(view("CUM"), every16("CUS"), view("ML"), MUL)
        mm(view("P2", 0, NL), view("WBG"), view("ZERO"), True, False)

        def eq(c):
            n = NL - 16 * c
            p1, o1 = PLACE["E16"][:2]
            p2, o2 = PLACE["CUM"][:2]
            node("v", [lambda: g.vector.tensor_scalar(T.EQ[:, c, 0:n], T[p1][:, o1 + 16 * c:o1 + NL], T[p2][:, o2 + c:o2 + c + 1], None, EQL)],
                 [view("E16", 16 * c, NL), view("CUM", c, c + 1)], [view("EQ", 256 * c, 256 * c + 256, ap=0)], cy(n / 2))
        for c in range(16):
            eq(c)
            if c < 15:
                mm(view("P2", 16 * c + 16, NL), view("WBG"), view("EQ", 256 * c, 256 * c + 256, ap=T.EQ[:, c, 16:NL - 16 * c]), False, False)
        mm(view("P2", 0, NL), view("WDG"), view("EQ", 0, NCELL, ap=T.EQ[:, :, 0:16]), False, True)
        lanes("P4", "WM16", ynew, "NMX", "MLS")
        tc(view("I1"), every16("MLS"))
        ts(view("I2"), view("I1"), 768, AND)
        tt(view("F1"), view("I2"), view("ILF"), ADD)
        tc(view("ZL"), view("F1"))
        ts(view("WC"), ynew, view("TH", t, t + 1), GE)
        lanes("P7", "B", view("WC"), "NM", "WIS")
        ts(view("W1"), every16("WIS"), 9.0, GE)
        if more:
            mm(view("P3", 0, 16), view("B"), view("ML"))
            an = A[t + 1]
            node("v", [lambda an=an: g.vector.tensor_reduce(an["ap"], T.P3[:, 0:16], AxisListType.X, ADD, negate=True)],
                 [view("P3", 0, 16)], [an], cy(16))
            cells(ynew, 256.0, an)
        tt(view("LD"), view("THD"), view("P2", 0, NL), GT)
        scan(view("LDS"), view("DJ"), view("LD"), 0.0, MUL, MAX)
        tt(view("LDL"), view("ML"), every16("LDS"), MUL)
        tt(SP, view("LDL"), view("W1"), MUL)
        tt(view("JL2"), every16("JLS"), SP, SUB)
        tc(view("JL2U"), view("JL2"))
        act(view(newrec), view("RS", 0, 2 * NCELL, 1, ("JL2U", 0, 16)))

        act(view("ZZ"), view(land, 0, N * NL, 1, ("ZL", 0, 16)), wait=("ar%d" % t, (N - 1) * neng))
        lanes("P4", "WM16", view("ZZ"), "NMX", "MZS")
        tc(view("I3"), every16("MZS"))
        ts(view("I4"), view("I3"), 4, SHR, 15, AND)
        tt(view("F2"), view("I4"), view("BSF"), ADD)
        tc(view("XL"), view("F2"))
        tc(view("X", 0, NCELL, 1, ("XL", 0, 16)), view("ZZ"))
        tc(view("RT", 0, NCELL, 1, ("XL", 0, 16)), view(newrec))
        ts(view("O1"), view("W1"), float(2 ** (3 - t)), MUL)
        tt(O2, view("O1"), every16("CUS"), ADD)
        tt(view("O3"), O2, view("TRF"), SUB)
        tt(view("M1"), view("LDL"), view("O3"), MUL)
        tt(view("M2"), view("M1"), view("TRF"), ADD)
        tc(view("VO"), view("M2"))
        tc(view("V", 0, VW, 1, ("VO", 0, 16)), ynew)
        if more:
            current(newrec)
        rec = newrec
        y = ynew

    dma("y", [(T.yx[:, :], T.X[:, :])], "oyx", [view("X")], [], 7.0)
    ts(view("EA"), view("O2A"), float(-DEAD), ADD)
    tt(view("EB"), view("EA"), view("SPA"), MUL)
    ts(view("EL", 16, 80), view("EB"), float(DEAD), ADD)
    tc(view("ELU"), view("EL"))
    tc(view("ELI"), view("EL"))
    ts(view("KI"), view("ELI"), 4, SHR)
    tc(view("KLU"), view("KI"))
    act(view("GV"), view("V", 0, VW, 1, ("ELU", 0, 80)))
    dma("y", [(T.yv[:, :], T.GV[:, :])], "oyv", [view("GV")], [])
    ts(view("CM"), view("V", 16, DEAD), 0.0, GE)
    scan(view("LOC", 16, DEAD), view("DM"), view("CM"), 0.0, MIN, ADD)
    act(view("LG"), view("LOC", 0, 4128, 1, ("ELU", 0, 80)))
    mms(view("P0", 0, NL), [(kset("KW", q), view("RT", 256 * q, 256 * q + 256)) for q in range(16)])
    act(view("GW"), view("P0", 0, NL))
    dma("y", [(T.yw[:, :], T.GW[:, :])], "oyw", [view("GW")], [])
    tc(view("SZ", 1, 257), view("LOC", 31, DEAD, 16))
    tc(view("SZS"), view("SZ", 0, 264, 1, ("E1L", 0, 16)))
    tc(view("SZH", 0, NL, 1, ("H0L", 0, 16)), view("SZS"))
    scan(view("PHI"), view("SZH"), view("NEG"), 0.0, ADD, MAX)
    tc(view("PHS"), view("PHI", 0, NL, 1, ("H0L", 0, 16)))
    tc(view("RH", 0, 264, 1, ("E1L", 0, 16)), view("PHS"))
    scan(view("PEI"), view("SZ", 1, 257), view("NEG"), -1.0, ADD, MAX)
    tt(view("RE", 1, 257), view("PEI"), view("SZ", 1, 257), SUB)
    tt(view("GE"), view("RE", 0, 264, 1, ("KLU", 0, 80)), view("LG"), ADD)
    dma("y", [(T.ye[:, :], T.GE[0::16, :])], "oye", [view("GE")], [])
    tt(view("GH"), view("RH", 0, 264, 1, ("KLU", 0, 80)), view("LG"), SUB)
    dma("y", [(T.yh[:, :], T.GH[0::16, :])], "oyh", [view("GH")], [])

    flush()
    for t in range(NR):
        g.wait_ge(T.sem["lo%d" % t], neng)
